import numpy as np, ml_dtypes
CORES = [24,32,56,88,96,104,30,38,62,94,102,110]
N = 12
KT, C = 2, 64
def setup_inputs(rng):
    return {"x": rng.standard_normal((N, 128, KT * C), dtype=np.float32).astype(ml_dtypes.bfloat16)}
def setup_inputs_big(rng):
    d = setup_inputs(rng)
    for k in ("x",): d[k] = (d[k].astype(np.float32) * 1024.0).astype(d[k].dtype)
    return d
def setup_inputs_small(rng):
    d = setup_inputs(rng)
    for k in ("x",): d[k] = (d[k].astype(np.float32) * (1 / 1024.0)).astype(d[k].dtype)
    return d
def setup_inputs_apart(rng):
    d = setup_inputs(rng)
    f = (10.0 ** rng.permutation(np.linspace(-1.5, 1.5, N))).astype(np.float32).reshape(N, 1, 1)
    for k in ("x",): d[k] = (d[k].astype(np.float32) * f).astype(d[k].dtype)
    return d
def reference(x):
    X = x.astype(np.float64)
    y = np.full((N, C, N * C), np.nan)
    for r in range(N):
        for i in range(N):
            s = i
            if s != r: y[r][:, C * i:C * i + C] = sum(X[r][:, C * t:C * t + C].T @ X[s][:, C * t:C * t + C] for t in range(KT))
    return {"y": y.astype(ml_dtypes.bfloat16 if x.dtype != np.float64 else np.float64)}

@@ -1,0 +1,168 @@
+from concourse.bass import DstId, RemoteDMATransfer
+
+C = 64
+KT = 2
+XW = KT * C
+NCHIP = 6
+PER = 2
+TW = PER * XW
+
+HOP1_ENGINES = 16
+HOP2_ENGINES = 8
+
+SCRATCH = {
+    "land": ("sbuf", [128, NCHIP * TW], "bfloat16"),
+    "ys": ("sbuf", [128, NCHIP * PER * C], "bfloat16"),
+}
+for _s in range(NCHIP):
+    SCRATCH["ps%d" % _s] = ("psum", [128, 512], "float32")
+
+SEMAPHORES = (["ld", "half", "sent", "cp", "st"] + ["arr%d" % s for s in range(NCHIP)]
+              + ["mm%d" % s for s in range(NCHIP)])
+
+
+def _engines(topo, src, dsts, n):
+    mask = topo.mask(src, dsts[0])
+    for d in dsts[1:]:
+        mask &= topo.mask(src, d)
+    out, k, b = 0, 0, 1
+    while b <= mask and k < n:
+        if mask & b:
+            out |= b
+            k += 1
+        b <<= 1
+    return out
+
+
+def _count(mask):
+    return bin(mask).count("1")
+
+
+def _perms(items):
+    if len(items) <= 1:
+        return [list(items)]
+    out = []
+    for i in range(len(items)):
+        for rest in _perms(items[:i] + items[i + 1:]):
+            out.append([items[i]] + rest)
+    return out
+
+
+def _links(topo, s, b):
+    a, d = topo.chip(s), topo.die(s)
+    if topo.mates(a, b):
+        return [("mate", a, d)]
+    if topo.same_plane(a, b):
+        return [("out", a, d), ("in", b, d)]
+    m = [k for k in range(topo.CHIPS) if topo.mates(a, k)][0]
+    return [("mate", a, d), ("out", m, d), ("in", b, d)]
+
+
+def _plan(T, topo):
+    cores = list(T.cores)
+    chips = []
+    for c in cores:
+        if topo.chip(c) not in chips:
+            chips.append(topo.chip(c))
+    members = dict((a, [c for c in cores if topo.chip(c) == a]) for a in chips)
+    relays = {}
+    for a in chips:
+        able = [k for k in range(topo.CHIPS * topo.CORES_PER_CHIP)
+                if topo.chip(k) == a and k not in cores and all(topo.may_write(k, d) for d in cores)]
+        relays[a] = able[:len(chips) - 1 - len(members[a])]
+    load, serves = {}, {}
+    for a in chips:
+        others = [b for b in chips if b != a]
+        best = None
+        for p in _perms(members[a] + relays[a]):
+            if not all(topo.may_write(s, d) for s, b in zip(p, others) for d in members[b]):
+                continue
+            l = dict(load)
+            for s, b in zip(p, others):
+                for k in _links(topo, s, b):
+                    l[k] = l.get(k, 0) + len(members[b])
+            key = (max(l.values()), sum(v * v for v in l.values()))
+            if best is None or key < best[0]:
+                best = (key, p, l)
+        load = best[2]
+        for s, b in zip(best[1], others):
+            serves[s] = b
+    return chips, members, relays, serves
+
+
+def _dst(topo, d):
+    a = topo.addr(d)
+    return DstId(rid=a[0], pnc=a[1])
+
+
+def rank_program(g, core, T, topo):
+    chips, members, relays, serves = _plan(T, topo)
+    chip = topo.chip(core)
+    if chip not in chips or core not in members[chip] + relays[chip]:
+        return
+    sem = T.sem
+    slot = chips.index(chip)
+    rank = T.rank_of(core)
+    tile = T.land[:, slot * TW:(slot + 1) * TW]
+    sent = 0
+    need = 0
+    for c in members[chip]:
+        if c != core:
+            need += _count(_engines(topo, c, relays[chip] + [k for k in members[chip] if k != c], HOP1_ENGINES))
+
+    if rank is not None:
+        h = members[chip].index(core)
+        own = T.land[:, slot * TW + h * XW: slot * TW + (h + 1) * XW]
+        g.sync.dma_start(own, T.x[:, :]).then_inc(sem.ld, 16)
+        g.wait_ge(sem.ld, 16)
+        dsts = relays[chip] + [c for c in members[chip] if c != core]
+        m1 = _engines(topo, core, dsts, HOP1_ENGINES)
+        g.remote_dma_fused([RemoteDMATransfer(dst_ids=[_dst(topo, d) for d in dsts], dma_engine_mask=m1,
+                                              remote_sem=sem.half, srcs=[own], dsts=[own for d in dsts], alu_op=0)],
+                           local_sem=sem.sent)
+        sent += _count(m1)
+
+    g.wait_ge(sem.half, need)
+    to = members[serves[core]]
+    m2 = _engines(topo, core, to, HOP2_ENGINES)
+    g.remote_dma_fused([RemoteDMATransfer(dst_ids=[_dst(topo, d) for d in to], dma_engine_mask=m2,
+                                          remote_sem=sem["arr%d" % slot], srcs=[tile], dsts=[tile for d in to],
+                                          alu_op=0)],
+                       local_sem=sem.sent)
+    sent += _count(m2)
+
+    if rank is not None:
+        te, ve = g.tensor, g.vector
+        sender = {}
+        for k in serves:
+            if serves[k] == chip:
+                sender[chips.index(topo.chip(k))] = k
+        order = [slot] + sorted(sender, key=lambda s: (T.rank_of(sender[s]) is None, s))
+        te.wait_ge(sem.ld, 16)
+        for s in order:
+            parts = list(range(len(members[chips[s]])))
+            if s == slot:
+                parts.sort(key=lambda k: k != h)
+            else:
+                te.wait_ge(sem["arr%d" % s], _count(_engines(topo, sender[s], members[chip], HOP2_ENGINES)))
+            for k in parts:
+                if s == slot and k != h:
+                    te.wait_ge(sem.half, need)
+                for t in range(KT):
+                    mm = te.matmul(T["ps%d" % s][0:C, k * C:(k + 1) * C],
+                                   T.land[:, slot * TW + h * XW + t * C: slot * TW + h * XW + (t + 1) * C],
+                                   T.land[:, s * TW + k * XW + t * C: s * TW + k * XW + (t + 1) * C],
+                                   t == 0, t == KT - 1)
+                mm.then_inc(sem["mm%d" % s], 1)
+        ncp = 0
+        for s in order:
+            ve.wait_ge(sem["mm%d" % s], len(members[chips[s]]))
+            for k, c in enumerate(members[chips[s]]):
+                r = T.rank_of(c)
+                ve.tensor_copy(T.ys[0:C, r * C:(r + 1) * C], T["ps%d" % s][0:C, k * C:(k + 1) * C]).then_inc(sem.cp, 1)
+                ncp += 1
+        g.sync.wait_ge(sem.cp, ncp)
+        g.sync.dma_start(T.y[:, :], T.ys[0:C, :]).then_inc(sem.st, 16)
+        g.sync.wait_ge(sem.st, 16)
+
+    g.wait_ge(sem.sent, sent)

@@ -9,16 +9,23 @@ TW = PER * XW
 
 HOP1_ENGINES = 16
 HOP2_ENGINES = 8
+RANK_CAP = 2
+RELAY_CAP = 1
+LATE = (0, 0, 0)
+SWEEPS = 1
 
 SCRATCH = {
+    "xd": ("dram", [128, XW], "bfloat16"),
     "land": ("sbuf", [128, NCHIP * TW], "bfloat16"),
     "ys": ("sbuf", [128, NCHIP * PER * C], "bfloat16"),
 }
 for _s in range(NCHIP):
     SCRATCH["ps%d" % _s] = ("psum", [128, 512], "float32")
 
-SEMAPHORES = (["ld", "half", "sent", "cp", "st"] + ["arr%d" % s for s in range(NCHIP)]
+SEMAPHORES = (["ldd", "ld", "half", "sent", "cp", "st"] + ["arr%d" % s for s in range(NCHIP)]
               + ["mm%d" % s for s in range(NCHIP)])
+
+_CACHE = {}
 
 
 def _engines(topo, src, dsts, n):
@@ -38,16 +45,6 @@ def _count(mask):
     return bin(mask).count("1")
 
 
-def _perms(items):
-    if len(items) <= 1:
-        return [list(items)]
-    out = []
-    for i in range(len(items)):
-        for rest in _perms(items[:i] + items[i + 1:]):
-            out.append([items[i]] + rest)
-    return out
-
-
 def _links(topo, s, b):
     a, d = topo.chip(s), topo.die(s)
     if topo.mates(a, b):
@@ -58,36 +55,78 @@ def _links(topo, s, b):
     return [("mate", a, d), ("out", m, d), ("in", b, d)]
 
 
+def _choices(cands, n):
+    if n == 0:
+        return [[]]
+    return [p + [s] for p in _choices(cands, n - 1) for s in cands[n - 1]]
+
+
+def _add(topo, l, s, d, w):
+    for k in _links(topo, s, topo.chip(d)):
+        l[k] = l.get(k, 0) + 1
+    for k in (("rank", d), ("late", topo.chip(d), topo.die(s))):
+        l[k] = l.get(k, 0) + w
+
+
 def _plan(T, topo):
     cores = list(T.cores)
+    if tuple(cores) in _CACHE:
+        return _CACHE[tuple(cores)]
     chips = []
     for c in cores:
         if topo.chip(c) not in chips:
             chips.append(topo.chip(c))
     members = dict((a, [c for c in cores if topo.chip(c) == a]) for a in chips)
-    relays = {}
+    able, options = {}, {}
     for a in chips:
-        able = [k for k in range(topo.CHIPS * topo.CORES_PER_CHIP)
-                if topo.chip(k) == a and k not in cores and all(topo.may_write(k, d) for d in cores)]
-        relays[a] = able[:len(chips) - 1 - len(members[a])]
-    load, serves = {}, {}
-    for a in chips:
+        able[a] = [k for k in range(topo.CHIPS * topo.CORES_PER_CHIP)
+                   if topo.chip(k) == a and k not in cores and all(topo.may_write(k, d) for d in cores)]
         others = [b for b in chips if b != a]
-        best = None
-        for p in _perms(members[a] + relays[a]):
-            if not all(topo.may_write(s, d) for s, b in zip(p, others) for d in members[b]):
-                continue
-            l = dict(load)
-            for s, b in zip(p, others):
-                for k in _links(topo, s, b):
-                    l[k] = l.get(k, 0) + len(members[b])
-            key = (max(l.values()), sum(v * v for v in l.values()))
-            if best is None or key < best[0]:
-                best = (key, p, l)
-        load = best[2]
-        for s, b in zip(best[1], others):
-            serves[s] = b
-    return chips, members, relays, serves
+        cands = [[s for s in members[a] + able[a] if all(topo.may_write(s, d) for d in members[b])] for b in others]
+        ok = [p for p in _choices(cands, len(others))
+              if not any(p.count(s) > (RANK_CAP if s in cores else RELAY_CAP) for s in p)]
+        few = min(len([s for s in able[a] if s in p]) for p in ok)
+        options[a] = []
+        for p in ok:
+            if len([s for s in able[a] if s in p]) == few:
+                for flip in _choices([[False, True] for m in members[a]], len(members[a])):
+                    seen, w = {}, []
+                    for s, b in zip(p, others):
+                        i = seen.get(s, 0)
+                        seen[s] = i + 1
+                        if s in cores and p.count(s) > 1 and flip[members[a].index(s)]:
+                            i = p.count(s) - 1 - i
+                        w.append((s, b, LATE[i] if s in cores else LATE[-1]))
+                    w.sort(key=lambda x: -x[2])
+                    if w not in options[a]:
+                        options[a].append(w)
+    chosen = {}
+    for sweep in range(SWEEPS):
+        for a in chips:
+            base = {}
+            for o in chosen:
+                if o != a:
+                    for s, d, w in chosen[o]:
+                        _add(topo, base, s, d, w)
+            best = None
+            for opt in options[a]:
+                l, res = dict(base), []
+                for s, b, w in opt:
+                    d = min(members[b], key=lambda d: (l.get(("rank", d), 0), topo.die(d) != topo.die(s)))
+                    _add(topo, l, s, d, w)
+                    res.append((s, d, w))
+                key = (max(l[k] for k in l if k[0] not in ("rank", "late")),
+                       max(l[k] for k in l if k[0] in ("rank", "late")), sum(v * v for v in l.values()))
+                if best is None or key < best[0]:
+                    best = (key, res)
+            chosen[a] = best[1]
+    serves, relays = {}, {}
+    for a in chips:
+        for s, d, w in sorted(chosen[a], key=lambda x: x[2]):
+            serves.setdefault(s, []).append(d)
+        relays[a] = [s for s in able[a] if s in serves]
+    _CACHE[tuple(cores)] = (chips, members, relays, serves)
+    return _CACHE[tuple(cores)]
 
 
 def _dst(topo, d):
@@ -96,55 +135,71 @@ def _dst(topo, d):
 
 
 def rank_program(g, core, T, topo):
+    if topo.chip(core) not in [topo.chip(c) for c in T.cores]:
+        return
     chips, members, relays, serves = _plan(T, topo)
     chip = topo.chip(core)
-    if chip not in chips or core not in members[chip] + relays[chip]:
+    if core not in members[chip] + relays[chip]:
         return
     sem = T.sem
     slot = chips.index(chip)
     rank = T.rank_of(core)
-    tile = T.land[:, slot * TW:(slot + 1) * TW]
     sent = 0
     need = 0
     for c in members[chip]:
         if c != core:
             need += _count(_engines(topo, c, relays[chip] + [k for k in members[chip] if k != c], HOP1_ENGINES))
 
+    def tile(s):
+        return T.land[:, s * TW:(s + 1) * TW]
+
+    def send(src, dst, dsts, engines, name):
+        m = _engines(topo, core, dsts, engines)
+        g.remote_dma_fused([RemoteDMATransfer(dst_ids=[_dst(topo, d) for d in dsts], dma_engine_mask=m,
+                                              remote_sem=sem[name], srcs=[src], dsts=[dst for d in dsts], alu_op=0)],
+                           local_sem=sem.sent)
+        return _count(m)
+
     if rank is not None:
         h = members[chip].index(core)
+        mates_here = [c for c in members[chip] if c != core]
         own = T.land[:, slot * TW + h * XW: slot * TW + (h + 1) * XW]
+        g.sync.dma_start(T.xd[:, :], T.x[:, :]).then_inc(sem.ldd, 16)
         g.sync.dma_start(own, T.x[:, :]).then_inc(sem.ld, 16)
+        g.wait_ge(sem.ldd, 16)
+        sent += send(T.xd[:, :], own, relays[chip] + mates_here, HOP1_ENGINES, "half")
         g.wait_ge(sem.ld, 16)
-        dsts = relays[chip] + [c for c in members[chip] if c != core]
-        m1 = _engines(topo, core, dsts, HOP1_ENGINES)
-        g.remote_dma_fused([RemoteDMATransfer(dst_ids=[_dst(topo, d) for d in dsts], dma_engine_mask=m1,
-                                              remote_sem=sem.half, srcs=[own], dsts=[own for d in dsts], alu_op=0)],
-                           local_sem=sem.sent)
-        sent += _count(m1)
 
     g.wait_ge(sem.half, need)
-    to = members[serves[core]]
-    m2 = _engines(topo, core, to, HOP2_ENGINES)
-    g.remote_dma_fused([RemoteDMATransfer(dst_ids=[_dst(topo, d) for d in to], dma_engine_mask=m2,
-                                          remote_sem=sem["arr%d" % slot], srcs=[tile], dsts=[tile for d in to],
-                                          alu_op=0)],
-                       local_sem=sem.sent)
-    sent += _count(m2)
+    sent += send(tile(slot), tile(slot), serves[core], HOP2_ENGINES, "arr%d" % slot)
 
     if rank is not None:
         te, ve = g.tensor, g.vector
-        sender = {}
+        ways = []
         for k in serves:
-            if serves[k] == chip:
-                sender[chips.index(topo.chip(k))] = k
-        order = [slot] + sorted(sender, key=lambda s: (T.rank_of(sender[s]) is None, s))
+            for i, d in enumerate(serves[k]):
+                if topo.chip(d) == chip:
+                    s = chips.index(topo.chip(k))
+                    when = 2 * i + (3 if T.rank_of(k) is None else 0)
+                    if d == core:
+                        ways.append((when, False, s, _count(_engines(topo, k, serves[k], HOP2_ENGINES))))
+                    else:
+                        ways.append((when + 1, True, s,
+                                     _count(_engines(topo, d, [c for c in members[chip] if c != d], HOP1_ENGINES))))
+        ways.sort()
+        for when, passed, s, n in ways:
+            if not passed:
+                g.wait_ge(sem["arr%d" % s], n)
+                sent += send(tile(s), tile(s), mates_here, HOP1_ENGINES, "arr%d" % s)
+
         te.wait_ge(sem.ld, 16)
-        for s in order:
+        order = [(slot, 0)] + [(w[2], w[3]) for w in ways]
+        for s, n in order:
             parts = list(range(len(members[chips[s]])))
             if s == slot:
                 parts.sort(key=lambda k: k != h)
             else:
-                te.wait_ge(sem["arr%d" % s], _count(_engines(topo, sender[s], members[chip], HOP2_ENGINES)))
+                te.wait_ge(sem["arr%d" % s], n)
             for k in parts:
                 if s == slot and k != h:
                     te.wait_ge(sem.half, need)
@@ -155,7 +210,7 @@ def rank_program(g, core, T, topo):
                                    t == 0, t == KT - 1)
                 mm.then_inc(sem["mm%d" % s], 1)
         ncp = 0
-        for s in order:
+        for s, n in order:
             ve.wait_ge(sem["mm%d" % s], len(members[chips[s]]))
             for k, c in enumerate(members[chips[s]]):
                 r = T.rank_of(c)

@@ -3,69 +3,33 @@ from concourse.bass import DstId, RemoteDMATransfer
 C = 64
 KT = 2
 XW = KT * C
-NCHIP = 6
-PER = 2
-TW = PER * XW
-
-HOP1_ENGINES = 16
-HOP2_ENGINES = 8
-RANK_CAP = 2
-RELAY_CAP = 1
-LATE = (0, 0, 0)
-SWEEPS = 1
+N = 12
+BANKS = 8
+FIRST = 2.5
 
 SCRATCH = {
     "xd": ("dram", [128, XW], "bfloat16"),
-    "land": ("sbuf", [128, NCHIP * TW], "bfloat16"),
-    "ys": ("sbuf", [128, NCHIP * PER * C], "bfloat16"),
+    "land": ("sbuf", [128, N * XW], "bfloat16"),
+    "ys": ("sbuf", [128, N * C], "bfloat16"),
 }
-for _s in range(NCHIP):
+for _s in range(BANKS):
     SCRATCH["ps%d" % _s] = ("psum", [128, 512], "float32")
 
-SEMAPHORES = (["ldd", "ld", "half", "sent", "cp", "st"] + ["arr%d" % s for s in range(NCHIP)]
-              + ["mm%d" % s for s in range(NCHIP)])
+SEMAPHORES = (["ldd", "ld", "sent", "st"] + ["arr%d" % s for s in range(N)]
+              + ["mm%d" % s for s in range(N)] + ["cp%d" % s for s in range(N)])
 
 _CACHE = {}
 
 
-def _engines(topo, src, dsts, n):
-    mask = topo.mask(src, dsts[0])
+def _mask(topo, src, dsts):
+    m = topo.mask(src, dsts[0])
     for d in dsts[1:]:
-        mask &= topo.mask(src, d)
-    out, k, b = 0, 0, 1
-    while b <= mask and k < n:
-        if mask & b:
-            out |= b
-            k += 1
-        b <<= 1
-    return out
+        m &= topo.mask(src, d)
+    return m
 
 
 def _count(mask):
     return bin(mask).count("1")
-
-
-def _links(topo, s, b):
-    a, d = topo.chip(s), topo.die(s)
-    if topo.mates(a, b):
-        return [("mate", a, d)]
-    if topo.same_plane(a, b):
-        return [("out", a, d), ("in", b, d)]
-    m = [k for k in range(topo.CHIPS) if topo.mates(a, k)][0]
-    return [("mate", a, d), ("out", m, d), ("in", b, d)]
-
-
-def _choices(cands, n):
-    if n == 0:
-        return [[]]
-    return [p + [s] for p in _choices(cands, n - 1) for s in cands[n - 1]]
-
-
-def _add(topo, l, s, d, w):
-    for k in _links(topo, s, topo.chip(d)):
-        l[k] = l.get(k, 0) + 1
-    for k in (("rank", d), ("late", topo.chip(d), topo.die(s))):
-        l[k] = l.get(k, 0) + w
 
 
 def _plan(T, topo):
@@ -77,55 +41,28 @@ def _plan(T, topo):
         if topo.chip(c) not in chips:
             chips.append(topo.chip(c))
     members = dict((a, [c for c in cores if topo.chip(c) == a]) for a in chips)
-    able, options = {}, {}
-    for a in chips:
-        able[a] = [k for k in range(topo.CHIPS * topo.CORES_PER_CHIP)
-                   if topo.chip(k) == a and k not in cores and all(topo.may_write(k, d) for d in cores)]
-        others = [b for b in chips if b != a]
-        cands = [[s for s in members[a] + able[a] if all(topo.may_write(s, d) for d in members[b])] for b in others]
-        ok = [p for p in _choices(cands, len(others))
-              if not any(p.count(s) > (RANK_CAP if s in cores else RELAY_CAP) for s in p)]
-        few = min(len([s for s in able[a] if s in p]) for p in ok)
-        options[a] = []
-        for p in ok:
-            if len([s for s in able[a] if s in p]) == few:
-                for flip in _choices([[False, True] for m in members[a]], len(members[a])):
-                    seen, w = {}, []
-                    for s, b in zip(p, others):
-                        i = seen.get(s, 0)
-                        seen[s] = i + 1
-                        if s in cores and p.count(s) > 1 and flip[members[a].index(s)]:
-                            i = p.count(s) - 1 - i
-                        w.append((s, b, LATE[i] if s in cores else LATE[-1]))
-                    w.sort(key=lambda x: -x[2])
-                    if w not in options[a]:
-                        options[a].append(w)
-    chosen = {}
-    for sweep in range(SWEEPS):
-        for a in chips:
-            base = {}
-            for o in chosen:
-                if o != a:
-                    for s, d, w in chosen[o]:
-                        _add(topo, base, s, d, w)
-            best = None
-            for opt in options[a]:
-                l, res = dict(base), []
-                for s, b, w in opt:
-                    d = min(members[b], key=lambda d: (l.get(("rank", d), 0), topo.die(d) != topo.die(s)))
-                    _add(topo, l, s, d, w)
-                    res.append((s, d, w))
-                key = (max(l[k] for k in l if k[0] not in ("rank", "late")),
-                       max(l[k] for k in l if k[0] in ("rank", "late")), sum(v * v for v in l.values()))
-                if best is None or key < best[0]:
-                    best = (key, res)
-            chosen[a] = best[1]
-    serves, relays = {}, {}
-    for a in chips:
-        for s, d, w in sorted(chosen[a], key=lambda x: x[2]):
-            serves.setdefault(s, []).append(d)
-        relays[a] = [s for s in able[a] if s in serves]
-    _CACHE[tuple(cores)] = (chips, members, relays, serves)
+    jobs, relays, when = {}, {}, {}
+    for c in cores:
+        a = topo.chip(c)
+        able = [k for k in range(topo.CHIPS * topo.CORES_PER_CHIP)
+                if topo.chip(k) == a and topo.die(k) == topo.die(c) and k not in cores
+                and all(topo.may_write(k, d) for d in cores)]
+        done = dict([(c, 0.0)] + [(k, FIRST) for k in able])
+        mine = dict((s, []) for s in done)
+        round_ = [chips[(chips.index(a) + j) % len(chips)] for j in range(1, len(chips))]
+        takers = [([d for d in members[b] if topo.die(d) == topo.die(c)] + members[b])[0] for b in round_]
+        takers.sort(key=lambda d: topo.may_write(c, d))
+        for d in takers:
+            s = min([s for s in [c] + able if topo.may_write(s, d)], key=lambda s: done[s])
+            done[s] += 1
+            mine[s].append(d)
+            when[(c, d)] = done[s]
+        relays[c] = [k for k in able if mine[k]]
+        relays[c].sort(key=lambda k: -len(mine[k]))
+        for s in mine:
+            if mine[s]:
+                jobs[s] = (c, mine[s])
+    _CACHE[tuple(cores)] = (members, jobs, relays, when)
     return _CACHE[tuple(cores)]
 
 
@@ -137,87 +74,82 @@ def _dst(topo, d):
 def rank_program(g, core, T, topo):
     if topo.chip(core) not in [topo.chip(c) for c in T.cores]:
         return
-    chips, members, relays, serves = _plan(T, topo)
-    chip = topo.chip(core)
-    if core not in members[chip] + relays[chip]:
+    members, jobs, relays, when = _plan(T, topo)
+    rank = T.rank_of(core)
+    if rank is None and core not in jobs:
         return
     sem = T.sem
-    slot = chips.index(chip)
-    rank = T.rank_of(core)
-    sent = 0
-    need = 0
-    for c in members[chip]:
-        if c != core:
-            need += _count(_engines(topo, c, relays[chip] + [k for k in members[chip] if k != c], HOP1_ENGINES))
 
-    def tile(s):
-        return T.land[:, s * TW:(s + 1) * TW]
+    def place(c):
+        r = T.rank_of(c)
+        return T.land[:, r * XW:(r + 1) * XW]
 
-    def send(src, dst, dsts, engines, name):
-        m = _engines(topo, core, dsts, engines)
-        g.remote_dma_fused([RemoteDMATransfer(dst_ids=[_dst(topo, d) for d in dsts], dma_engine_mask=m,
-                                              remote_sem=sem[name], srcs=[src], dsts=[dst for d in dsts], alu_op=0)],
-                           local_sem=sem.sent)
-        return _count(m)
+    def transfer(src, c, dsts, m):
+        return RemoteDMATransfer(dst_ids=[_dst(topo, d) for d in dsts], dma_engine_mask=m,
+                                 remote_sem=sem["arr%d" % T.rank_of(c)], srcs=[src], dsts=[place(c) for d in dsts],
+                                 alu_op=0)
 
-    if rank is not None:
-        h = members[chip].index(core)
-        mates_here = [c for c in members[chip] if c != core]
-        own = T.land[:, slot * TW + h * XW: slot * TW + (h + 1) * XW]
-        g.sync.dma_start(T.xd[:, :], T.x[:, :]).then_inc(sem.ldd, 16)
-        g.sync.dma_start(own, T.x[:, :]).then_inc(sem.ld, 16)
-        g.wait_ge(sem.ldd, 16)
-        sent += send(T.xd[:, :], own, relays[chip] + mates_here, HOP1_ENGINES, "half")
-        g.wait_ge(sem.ld, 16)
+    def masks(c):
+        here = relays[c] + [k for k in members[topo.chip(c)] if k != c]
+        off = _mask(topo, c, jobs[c][1]) if c in jobs else 0
+        return off, _mask(topo, c, here) & ~off
 
-    g.wait_ge(sem.half, need)
-    sent += send(tile(slot), tile(slot), serves[core], HOP2_ENGINES, "arr%d" % slot)
+    if rank is None:
+        c, dsts = jobs[core]
+        g.wait_ge(sem["arr%d" % T.rank_of(c)], _count(masks(c)[1]))
+        m = _mask(topo, core, dsts)
+        g.remote_dma_fused([transfer(place(c), c, dsts, m)], local_sem=sem.sent)
+        g.wait_ge(sem.sent, _count(m))
+        return
 
-    if rank is not None:
-        te, ve = g.tensor, g.vector
-        ways = []
-        for k in serves:
-            for i, d in enumerate(serves[k]):
-                if topo.chip(d) == chip:
-                    s = chips.index(topo.chip(k))
-                    when = 2 * i + (3 if T.rank_of(k) is None else 0)
-                    if d == core:
-                        ways.append((when, False, s, _count(_engines(topo, k, serves[k], HOP2_ENGINES))))
-                    else:
-                        ways.append((when + 1, True, s,
-                                     _count(_engines(topo, d, [c for c in members[chip] if c != d], HOP1_ENGINES))))
-        ways.sort()
-        for when, passed, s, n in ways:
-            if not passed:
-                g.wait_ge(sem["arr%d" % s], n)
-                sent += send(tile(s), tile(s), mates_here, HOP1_ENGINES, "arr%d" % s)
+    chip = topo.chip(core)
+    others_here = [c for c in members[chip] if c != core]
+    g.sync.dma_start(T.xd[:, :], T.x[:, :]).then_inc(sem.ldd, 16)
+    g.sync.dma_start(place(core), T.x[:, :]).then_inc(sem.ld, 16)
+    g.wait_ge(sem.ldd, 16)
+    off, on = masks(core)
+    first = [transfer(T.xd[:, :], core, relays[core] + others_here, on)]
+    if core in jobs:
+        first.append(transfer(T.xd[:, :], core, jobs[core][1], off))
+    g.remote_dma_fused(first, local_sem=sem.sent)
+    sent = _count(on) + (_count(off) if core in jobs else 0)
 
-        te.wait_ge(sem.ld, 16)
-        order = [(slot, 0)] + [(w[2], w[3]) for w in ways]
-        for s, n in order:
-            parts = list(range(len(members[chips[s]])))
-            if s == slot:
-                parts.sort(key=lambda k: k != h)
-            else:
-                te.wait_ge(sem["arr%d" % s], n)
-            for k in parts:
-                if s == slot and k != h:
-                    te.wait_ge(sem.half, need)
-                for t in range(KT):
-                    mm = te.matmul(T["ps%d" % s][0:C, k * C:(k + 1) * C],
-                                   T.land[:, slot * TW + h * XW + t * C: slot * TW + h * XW + (t + 1) * C],
-                                   T.land[:, s * TW + k * XW + t * C: s * TW + k * XW + (t + 1) * C],
-                                   t == 0, t == KT - 1)
-                mm.then_inc(sem["mm%d" % s], 1)
-        ncp = 0
-        for s, n in order:
-            ve.wait_ge(sem["mm%d" % s], len(members[chips[s]]))
-            for k, c in enumerate(members[chips[s]]):
-                r = T.rank_of(c)
-                ve.tensor_copy(T.ys[0:C, r * C:(r + 1) * C], T["ps%d" % s][0:C, k * C:(k + 1) * C]).then_inc(sem.cp, 1)
-                ncp += 1
-        g.sync.wait_ge(sem.cp, ncp)
-        g.sync.dma_start(T.y[:, :], T.ys[0:C, :]).then_inc(sem.st, 16)
-        g.sync.wait_ge(sem.st, 16)
+    ways = [(0.5, True, c, _count(masks(c)[1])) for c in others_here]
+    fwd = _mask(topo, core, others_here)
+    for s in jobs:
+        c, dsts = jobs[s]
+        for d in dsts:
+            if d == core:
+                ways.append((when[(c, d)], False, c, _count(_mask(topo, s, dsts))))
+            elif topo.chip(d) == chip:
+                ways.append((when[(c, d)] + 1, True, c, _count(_mask(topo, d, [k for k in members[chip] if k != d]))))
+    ways.sort()
+    for t, passed, c, n in ways:
+        if not passed:
+            g.wait_ge(sem["arr%d" % T.rank_of(c)], n)
+            g.remote_dma_fused([transfer(place(c), c, others_here, fwd)], local_sem=sem.sent)
+            sent += _count(fwd)
 
+    te, ve = g.tensor, g.vector
+    te.wait_ge(sem.ld, 16)
+    for i, (t, passed, c, n) in enumerate(ways):
+        r = T.rank_of(c)
+        te.wait_ge(sem["arr%d" % r], n)
+        if i >= BANKS:
+            te.wait_ge(sem["cp%d" % T.rank_of(ways[i - BANKS][2])], 1)
+        for k in range(KT):
+            mm = te.matmul(T["ps%d" % (i % BANKS)][0:C, 0:C],
+                           T.land[:, rank * XW + k * C: rank * XW + (k + 1) * C],
+                           T.land[:, r * XW + k * C: r * XW + (k + 1) * C], k == 0, k == KT - 1)
+        mm.then_inc(sem["mm%d" % r], 1)
+    for i, (t, passed, c, n) in enumerate(ways):
+        r = T.rank_of(c)
+        ve.wait_ge(sem["mm%d" % r], 1)
+        ve.tensor_copy(T.ys[0:C, r * C:(r + 1) * C], T["ps%d" % (i % BANKS)][0:C, 0:C]).then_inc(sem["cp%d" % r], 1)
+    for i, (t, passed, c, n) in enumerate(ways):
+        r = T.rank_of(c)
+        q = (g.sync, g.scalar)[i % 2]
+        q.wait_ge(sem["cp%d" % r], 1)
+        q.dma_start(T.y[:, r * C:(r + 1) * C], T.ys[0:C, r * C:(r + 1) * C]).then_inc(sem.st, 16)
+    g.sync.wait_ge(sem.st, 16 * len(ways))
     g.wait_ge(sem.sent, sent)

from concourse.bass import DstId, RemoteDMATransfer

C = 64
KT = 2
XW = KT * C
N = 12
BANKS = 8
FIRST = 2.5

SCRATCH = {
    "xd": ("dram", [128, XW], "bfloat16"),
    "land": ("sbuf", [128, N * XW], "bfloat16"),
    "ys": ("sbuf", [128, N * C], "bfloat16"),
}
for _s in range(BANKS):
    SCRATCH["ps%d" % _s] = ("psum", [128, 512], "float32")

SEMAPHORES = (["ldd", "ld", "sent", "st"] + ["arr%d" % s for s in range(N)]
              + ["mm%d" % s for s in range(N)] + ["cp%d" % s for s in range(N)])

_CACHE = {}


def _mask(topo, src, dsts):
    m = topo.mask(src, dsts[0])
    for d in dsts[1:]:
        m &= topo.mask(src, d)
    return m


def _count(mask):
    return bin(mask).count("1")


def _plan(T, topo):
    cores = list(T.cores)
    if tuple(cores) in _CACHE:
        return _CACHE[tuple(cores)]
    chips = []
    for c in cores:
        if topo.chip(c) not in chips:
            chips.append(topo.chip(c))
    members = dict((a, [c for c in cores if topo.chip(c) == a]) for a in chips)
    jobs, relays, when = {}, {}, {}
    for c in cores:
        a = topo.chip(c)
        able = [k for k in range(topo.CHIPS * topo.CORES_PER_CHIP)
                if topo.chip(k) == a and topo.die(k) == topo.die(c) and k not in cores
                and all(topo.may_write(k, d) for d in cores)]
        done = dict([(c, 0.0)] + [(k, FIRST) for k in able])
        mine = dict((s, []) for s in done)
        round_ = [chips[(chips.index(a) + j) % len(chips)] for j in range(1, len(chips))]
        takers = [([d for d in members[b] if topo.die(d) == topo.die(c)] + members[b])[0] for b in round_]
        takers.sort(key=lambda d: topo.may_write(c, d))
        for d in takers:
            s = min([s for s in [c] + able if topo.may_write(s, d)], key=lambda s: done[s])
            done[s] += 1
            mine[s].append(d)
            when[(c, d)] = done[s]
        relays[c] = [k for k in able if mine[k]]
        relays[c].sort(key=lambda k: -len(mine[k]))
        for s in mine:
            if mine[s]:
                jobs[s] = (c, mine[s])
    _CACHE[tuple(cores)] = (members, jobs, relays, when)
    return _CACHE[tuple(cores)]


def _dst(topo, d):
    a = topo.addr(d)
    return DstId(rid=a[0], pnc=a[1])


def rank_program(g, core, T, topo):
    if topo.chip(core) not in [topo.chip(c) for c in T.cores]:
        return
    members, jobs, relays, when = _plan(T, topo)
    rank = T.rank_of(core)
    if rank is None and core not in jobs:
        return
    sem = T.sem

    def place(c):
        r = T.rank_of(c)
        return T.land[:, r * XW:(r + 1) * XW]

    def transfer(src, c, dsts, m):
        return RemoteDMATransfer(dst_ids=[_dst(topo, d) for d in dsts], dma_engine_mask=m,
                                 remote_sem=sem["arr%d" % T.rank_of(c)], srcs=[src], dsts=[place(c) for d in dsts],
                                 alu_op=0)

    def masks(c):
        here = relays[c] + [k for k in members[topo.chip(c)] if k != c]
        off = _mask(topo, c, jobs[c][1]) if c in jobs else 0
        return off, _mask(topo, c, here) & ~off

    if rank is None:
        c, dsts = jobs[core]
        g.wait_ge(sem["arr%d" % T.rank_of(c)], _count(masks(c)[1]))
        m = _mask(topo, core, dsts)
        g.remote_dma_fused([transfer(place(c), c, dsts, m)], local_sem=sem.sent)
        g.wait_ge(sem.sent, _count(m))
        return

    chip = topo.chip(core)
    others_here = [c for c in members[chip] if c != core]
    g.sync.dma_start(T.xd[:, :], T.x[:, :]).then_inc(sem.ldd, 16)
    g.sync.dma_start(place(core), T.x[:, :]).then_inc(sem.ld, 16)
    g.wait_ge(sem.ldd, 16)
    off, on = masks(core)
    first = [transfer(T.xd[:, :], core, relays[core] + others_here, on)]
    if core in jobs:
        first.append(transfer(T.xd[:, :], core, jobs[core][1], off))
    g.remote_dma_fused(first, local_sem=sem.sent)
    sent = _count(on) + (_count(off) if core in jobs else 0)

    ways = [(0.5, True, c, _count(masks(c)[1])) for c in others_here]
    fwd = _mask(topo, core, others_here)
    for s in jobs:
        c, dsts = jobs[s]
        for d in dsts:
            if d == core:
                ways.append((when[(c, d)], False, c, _count(_mask(topo, s, dsts))))
            elif topo.chip(d) == chip:
                ways.append((when[(c, d)] + 1, True, c, _count(_mask(topo, d, [k for k in members[chip] if k != d]))))
    ways.sort()
    for t, passed, c, n in ways:
        if not passed:
            g.wait_ge(sem["arr%d" % T.rank_of(c)], n)
            g.remote_dma_fused([transfer(place(c), c, others_here, fwd)], local_sem=sem.sent)
            sent += _count(fwd)

    te, ve = g.tensor, g.vector
    te.wait_ge(sem.ld, 16)
    for i, (t, passed, c, n) in enumerate(ways):
        r = T.rank_of(c)
        te.wait_ge(sem["arr%d" % r], n)
        if i >= BANKS:
            te.wait_ge(sem["cp%d" % T.rank_of(ways[i - BANKS][2])], 1)
        for k in range(KT):
            mm = te.matmul(T["ps%d" % (i % BANKS)][0:C, 0:C],
                           T.land[:, rank * XW + k * C: rank * XW + (k + 1) * C],
                           T.land[:, r * XW + k * C: r * XW + (k + 1) * C], k == 0, k == KT - 1)
        mm.then_inc(sem["mm%d" % r], 1)
    for i, (t, passed, c, n) in enumerate(ways):
        r = T.rank_of(c)
        ve.wait_ge(sem["mm%d" % r], 1)
        ve.tensor_copy(T.ys[0:C, r * C:(r + 1) * C], T["ps%d" % (i % BANKS)][0:C, 0:C]).then_inc(sem["cp%d" % r], 1)
    for i, (t, passed, c, n) in enumerate(ways):
        r = T.rank_of(c)
        q = (g.sync, g.scalar)[i % 2]
        q.wait_ge(sem["cp%d" % r], 1)
        q.dma_start(T.y[:, r * C:(r + 1) * C], T.ys[0:C, r * C:(r + 1) * C]).then_inc(sem.st, 16)
    g.sync.wait_ge(sem.st, 16 * len(ways))
    g.wait_ge(sem.sent, sent)
